import numpy as np
import ml_dtypes


def mxq(x, axis, fmt="e4m3"):
    dtype, down = {"e4m3": (ml_dtypes.float8_e4m3fn, 7), "e5m2": (ml_dtypes.float8_e5m2, 14)}[fmt]
    v = np.moveaxis(np.asarray(x, np.float32).astype(ml_dtypes.bfloat16).astype(np.float64), axis, -1)
    blocks = v.reshape(v.shape[:-1] + (-1, 32))
    amax = np.abs(blocks).max(-1, keepdims=True)
    byte = np.maximum(np.where(amax > 0, np.frexp(amax)[1] - 1 + 127, 0) - down, 1)
    scale = np.exp2(byte - 127.0)
    codes = (blocks / scale).astype(np.float32).astype(dtype).astype(np.float64)
    return np.moveaxis((codes * scale).reshape(v.shape), -1, axis)


WIDE = False


def mx_kscale(k):
    if not WIDE:
        return np.ones(k)
    levels = np.array([10, -10, 5, -5, 0])
    if k % 512:
        return np.exp2(np.random.permutation(np.resize(levels, k // 32))).repeat(32)
    a = np.empty((k // 512, 16))
    for p in range(k // 512):
        a[p, :8] = np.random.permutation(np.resize(levels, 8))
        for g in range(8):
            far = levels[np.abs(levels - a[p, g]) >= 10]
            a[p, g + 8] = far[np.random.randint(len(far))]
    return np.exp2(a.ravel()).repeat(32)


def f64(x):
    return np.asarray(x).astype(np.float64)


def striped(idx):
    return np.tile(idx.reshape(-1, 16).T, (8, 1)).astype(np.uint16)


def unstriped(offs):
    return offs[:16].T.reshape(-1).astype(np.int64)


E2M1 = np.array([0.0, 0.5, 1.0, 1.5, 2.0, 3.0, 4.0, 6.0, -0.0, -0.5, -1.0, -1.5, -2.0, -3.0, -4.0, -6.0])


def pack_weight(w, fmt):
    k, n = w.shape
    w = f64(np.asarray(w, np.float32).astype(ml_dtypes.bfloat16)).reshape(k // 32, 32, n)
    amax = np.abs(w).max(1)
    if fmt == "e4m3":
        byte = np.frexp(amax)[1] - 1 + 127 - 7
    else:
        mant, ex = np.frexp(amax / 6.0)
        byte = np.where(mant > 0.5, ex, ex - 1) + 127
    byte = np.clip(np.where(amax > 0, byte, 1), 1, 254)
    scaled = (w * np.exp2(127.0 - byte)[:, None, :]).reshape(k, n).astype(np.float32)
    by_word = np.ascontiguousarray(scaled.reshape(k // 512, 128, 4, n).transpose(0, 1, 3, 2))
    if fmt == "e4m3":
        words = by_word.astype(ml_dtypes.float8_e4m3fn).view(np.uint8)
    else:
        c = by_word.astype(ml_dtypes.float4_e2m1fn).view(np.uint8) & 0xF
        words = (c[..., 0::2] | (c[..., 1::2] << 4)).reshape(k // 512, 128, 2 * n)
    return np.ascontiguousarray(words), np.ascontiguousarray(byte.astype(np.uint8).reshape(k // 512, 16, n))


def unpack_weight(words, scales, fmt):
    g, _, n = scales.shape
    words = np.ascontiguousarray(words).reshape(g, 128, n, -1)
    if fmt == "e4m3":
        vals = words.view(ml_dtypes.float8_e4m3fn).astype(np.float64)
    else:
        nib = np.empty((g, 128, n, 4), np.uint8)
        nib[..., 0::2] = words & 0xF
        nib[..., 1::2] = words >> 4
        vals = E2M1[nib]
    vals = vals * np.repeat(np.exp2(scales.astype(np.float64) - 127.0), 8, axis=1)[..., None]
    return vals.transpose(0, 1, 3, 2).reshape(g * 512, n)


def gelu(v):
    return 0.5 * v * (1.0 + np.tanh(np.sqrt(2.0 / np.pi) * (v + 0.044715 * v**3)))


K, T, E, N = 2048, 1536, 8, 128
COUNTS = (128, 128, 128, 128, 128, 384, 384, 128)
STARTS = np.cumsum((0,) + COUNTS)


def by_expert(wq, xq):
    return np.concatenate([wq[e].T @ xq[:, STARTS[e]:STARTS[e + 1]] for e in range(E)], axis=1)


def setup_inputs():
    n = np.random.standard_normal
    s = mx_kscale(K)[:, None]
    expert = np.random.permutation(np.repeat(np.arange(E), COUNTS))
    slot_token = np.argsort(expert, kind="stable")
    w = [pack_weight(m, "e2m1") for m in n((E, K, N)) / np.sqrt(K) / s[None]]
    return {
        "xT": (n((K, T)) * s).astype(np.float32),
        "w_words": np.stack([m[0] for m in w]),
        "w_scales": np.stack([m[1] for m in w]),
        "b": (0.3 * n((N, E))).astype(np.float32),
        "gate": np.tile(np.random.uniform(0.2, 1.0, T), (N, 1)).astype(np.float32),
        "offs": striped(slot_token),
    }


def reference(xT, w_words, w_scales, b, gate, offs):
    idx = unstriped(offs)
    w = np.stack([unpack_weight(w_words[e], w_scales[e], "e2m1") for e in range(E)])
    xq = mxq(f64(xT)[:, idx], 0, "e4m3")
    y = by_expert(w, xq)
    y = gelu(y + np.repeat(f64(b), COUNTS, axis=1))
    out = np.zeros((N, T))
    out[:, idx] = f64(gate) * y
    return out

@@ -1,0 +1,138 @@
+import concourse.mybir as mybir
+
+F32 = mybir.dt.float32
+BF16 = mybir.dt.bfloat16
+I32 = mybir.dt.int32
+U32 = mybir.dt.uint32
+U16 = mybir.dt.uint16
+U8 = mybir.dt.uint8
+FP8X4 = mybir.dt.float8_e4m3fn_x4
+FP4X4 = mybir.dt.float4_e2m1fn_x4
+ACT = mybir.ActivationFunctionType
+MULT = mybir.AluOpType.mult
+
+P = 128
+K, T, E, N = 2048, 1536, 8, 128
+COUNTS = (128, 128, 128, 128, 128, 384, 384, 128)
+PASSES = K // 512
+FLOPS = 2 * K * N * T
+
+
+def tile_moe_rag_lin_gelu_kernel(tc, xT, w_words, w_scales, b, gate, offs, out):
+    nc = tc.nc
+    with (
+        tc.tile_pool(name="held", bufs=1) as held,
+        tc.psum_pool(name="psum", bufs=1) as psum,
+    ):
+        offsets = held.tile([P, T // 16], U16, name="offsets")
+        wscale = held.tile([P, E * PASSES, N], U8, name="wscale", align_bytes=64)
+        words = held.tile([P, E * PASSES, 2 * N], U8, name="words", align_bytes=64)
+        bias = held.tile([P, E], F32, name="bias")
+        gates = held.tile([P, T], F32, name="gates")
+        warm = held.tile([P, 1], F32, name="warm")
+        packed = held.tile([P, T], U8, name="packed", align_bytes=64)
+        last = held.tile([P, T], U8, name="last", align_bytes=64)
+        gpacked = held.tile([P, T], U8, name="gpacked", align_bytes=64)
+        codes = [held.tile([P, T], U32, name=f"codes{a}", align_bytes=64) for a in range(PASSES)]
+        gscales = [gpacked] + [held.tile([P, T], U8, name=f"gscales{a}", align_bytes=64) for a in range(1, PASSES)]
+        gcodes = [held.tile([P, T], U32, name=f"gcodes{a}", align_bytes=64) for a in range(PASSES)]
+        y = held.tile([P, T], F32, name="y")
+        result = held.tile([P, T], F32, name="result")
+        banks = [psum.tile([P, 512], F32, name=f"bank{i}") for i in range(3)]
+
+        chunks = []
+        for a in range(PASSES):
+            for c in range(3):
+                if a == PASSES - 1 and c == 2:
+                    chunks.append((a, c * 512, 256, "s"))
+                    chunks.append((a, c * 512 + 256, 256, "v"))
+                else:
+                    chunks.append((a, c * 512, 512, "v" if (a, c) == (0, 1) else "s"))
+
+        nc.vector.memset(warm[:], 0.0)
+        nc.scalar.activation(warm[:], warm[:], ACT.Gelu_apprx_tanh)
+        nc.gpsimd.memset(packed[:].bitcast(I32), 0)
+        nc.gpsimd.memset(wscale[:].rearrange("p c n -> p (c n)").bitcast(I32), 0)
+        for tile in (last, gscales[1], gscales[2]):
+            nc.gpsimd.memset(tile[:].bitcast(I32), 0)
+        ws32 = w_scales.bitcast(I32)
+        raws = []
+        for i, (a, t0, w, eng) in enumerate(chunks):
+            raw = held.tile([P, 4, w], F32, name=f"raw{i}")
+            nc.sync.dma_start(out=raw[:], in_=xT[512 * a : 512 * (a + 1), t0 : t0 + w].rearrange("(p j) w -> p j w", j=4))
+            raws.append(raw)
+            if i == 1:
+                nc.sync.dma_start(offsets[:], offs)
+            if i == 2:
+                for q in range(4):
+                    nc.sync.dma_start(
+                        out=wscale[32 * q : 32 * q + 4, :, :].bitcast(I32),
+                        in_=ws32[:, :, 4 * q : 4 * q + 4, :].rearrange("e a q n -> q (e a) n"),
+                    )
+        ww32 = w_words.bitcast(I32)
+        for h in range(4):
+            nc.sync.dma_start(
+                out=words[:, 8 * h : 8 * h + 8, :].bitcast(I32),
+                in_=ww32[2 * h : 2 * h + 2, :, :, :].rearrange("e a p n -> p (e a) n"),
+            )
+        nc.sync.dma_start(out=bias[:], in_=b)
+        nc.sync.dma_start(out=gates[:], in_=gate)
+
+        def gather(a, s0, s1):
+            idx = offsets[:, s0 // 16 : s1 // 16]
+            nc.vector.tensor_copy(gcodes[a][:, s0:s1], codes[a][:].indirect(idx))
+            if a >= 2:
+                dst, src = (gpacked, packed) if a == 2 else (gscales[3], last)
+                nc.vector.tensor_copy(dst[:, s0:s1], src[:].indirect(idx))
+
+        def quantise(i):
+            a, t0, w, eng = chunks[i]
+            grouped = held.tile([P, w, 4], BF16, name=f"grouped{i}", align_bytes=64)
+            dst = grouped[:].rearrange("p (c i) t -> p c t i", i=4)
+            src = raws[i][:].rearrange("p t (c i) -> p c t i", i=4)
+            if eng == "s":
+                nc.scalar.activation(dst, src, ACT.Copy)
+            else:
+                nc.vector.tensor_copy(dst, src)
+            nc.vector.quantize_mx(
+                out=codes[a][:, t0 : t0 + w].bitcast(FP8X4),
+                scales=(last[:, t0 : t0 + w] if a == 3 else packed[4 * a :, t0 : t0 + w]),
+                in_=grouped[:].rearrange("p w t -> p (w t)"),
+            )
+
+        for i in range(len(chunks)):
+            quantise(i)
+            a, t0, w, eng = chunks[i]
+            if t0 + w == T and a < PASSES - 1:
+                gather(a, 0, 768)
+                gather(a, 768, 1536)
+
+        for a in (1, 2):
+            nc.sync.dma_start(out=gscales[a][0:112, :].bitcast(I32), in_=gpacked[4 * a : 4 * a + 112, :].bitcast(I32))
+
+        expert = [e for e in range(E) for _ in range(COUNTS[e] // 128)]
+        starts = [sum(COUNTS[:e]) for e in range(E + 1)]
+        for i in range(3):
+            s0, s1 = 512 * i, 512 * i + 512
+            gather(PASSES - 1, s0, s1)
+            for g in range(4 * i, 4 * i + 4):
+                e = expert[g]
+                cols = slice(128 * g, 128 * g + 128)
+                for a in range(PASSES):
+                    nc.tensor.matmul_mx(
+                        out=banks[i][:, 128 * (g - 4 * i) : 128 * (g - 4 * i) + 128],
+                        lhsT=words[:, PASSES * e + a, :].bitcast(FP4X4),
+                        lhsT_scale=wscale[:, PASSES * e + a, :],
+                        rhs=gcodes[a][:, cols].bitcast(FP8X4),
+                        rhs_scale=gscales[a][:, cols],
+                        start=(a == 0),
+                        stop=(a == PASSES - 1),
+                    )
+            for e in range(E):
+                lo, hi = max(starts[e], s0), min(starts[e + 1], s1)
+                if lo < hi:
+                    nc.scalar.activation(y[:, lo:hi], banks[i][:, lo - s0 : hi - s0], ACT.Gelu_apprx_tanh, bias=bias[:, e : e + 1])
+        for i in range(3):
+            s0, s1 = 512 * i, 512 * i + 512
+            nc.vector.tensor_tensor(result[:].indirect(offsets[:, s0 // 16 : s1 // 16]), y[:, s0:s1], gates[:, s0:s1], MULT)
+        nc.sync.dma_start(out=out, in_=result[:])

@@ -17,6 +17,20 @@ COUNTS = (128, 128, 128, 128, 128, 384, 384, 128)
 PASSES = K // 512
 FLOPS = 2 * K * N * T
 
+LOADS = (
+    (0, 0, 512), (0, 512, 512), (0, 1024, 512),
+    (1, 0, 512), (1, 512, 512), (1, 1024, 512),
+    (2, 0, 512), (2, 512, 512), (2, 1024, 512),
+    (3, 0, 512), (3, 512, 512), (3, 1024, 256), (3, 1280, 256),
+)
+UNITS = (
+    (0, 0, 512, "s"), (0, 512, 512, "s"), (0, 1024, 256, "s"), (0, 1280, 256, "v"),
+    (1, 0, 512, "s"), (1, 512, 512, "s"), (1, 1024, 256, "s"), (1, 1280, 256, "v"),
+    (2, 0, 512, "s"), (2, 512, 512, "s"), (2, 1024, 256, "s"), (2, 1280, 256, "v"),
+    (3, 0, 512, "s"), (3, 512, 512, "s"), (3, 1024, 256, "s"), (3, 1280, 128, "s"), (3, 1408, 128, "v"),
+)
+SLICES = ((0, 256), (256, 896), (896, 1536))
+
 
 def tile_moe_rag_lin_gelu_kernel(tc, xT, w_words, w_scales, b, gate, offs, out):
     nc = tc.nc
@@ -31,96 +45,101 @@ def tile_moe_rag_lin_gelu_kernel(tc, xT, w_words, w_scales, b, gate, offs, out):
         gates = held.tile([P, T], F32, name="gates")
         warm = held.tile([P, 1], F32, name="warm")
         packed = held.tile([P, T], U8, name="packed", align_bytes=64)
-        last = held.tile([P, T], U8, name="last", align_bytes=64)
         gpacked = held.tile([P, T], U8, name="gpacked", align_bytes=64)
+        moved = [held.tile([P, T], U8, name=f"moved{a}", align_bytes=64) for a in range(3)]
+        ROW = (4, 8, 12, 0)
         codes = [held.tile([P, T], U32, name=f"codes{a}", align_bytes=64) for a in range(PASSES)]
-        gscales = [gpacked] + [held.tile([P, T], U8, name=f"gscales{a}", align_bytes=64) for a in range(1, PASSES)]
         gcodes = [held.tile([P, T], U32, name=f"gcodes{a}", align_bytes=64) for a in range(PASSES)]
+        gscales = moved + [gpacked]
         y = held.tile([P, T], F32, name="y")
+        z = held.tile([P, T], F32, name="z")
         result = held.tile([P, T], F32, name="result")
         banks = [psum.tile([P, 512], F32, name=f"bank{i}") for i in range(3)]
-
-        chunks = []
-        for a in range(PASSES):
-            for c in range(3):
-                if a == PASSES - 1 and c == 2:
-                    chunks.append((a, c * 512, 256, "s"))
-                    chunks.append((a, c * 512 + 256, 256, "v"))
-                else:
-                    chunks.append((a, c * 512, 512, "v" if (a, c) == (0, 1) else "s"))
 
         nc.vector.memset(warm[:], 0.0)
         nc.scalar.activation(warm[:], warm[:], ACT.Gelu_apprx_tanh)
         nc.gpsimd.memset(packed[:].bitcast(I32), 0)
         nc.gpsimd.memset(wscale[:].rearrange("p c n -> p (c n)").bitcast(I32), 0)
-        for tile in (last, gscales[1], gscales[2]):
+        for tile in moved:
             nc.gpsimd.memset(tile[:].bitcast(I32), 0)
         ws32 = w_scales.bitcast(I32)
-        raws = []
-        for i, (a, t0, w, eng) in enumerate(chunks):
+        ww32 = w_words.bitcast(I32)
+
+        def load_scales():
+            for q in range(4):
+                nc.sync.dma_start(
+                    out=wscale[32 * q : 32 * q + 4, :, :].bitcast(I32),
+                    in_=ws32[:, :, 4 * q : 4 * q + 4, :].rearrange("e a q n -> q (e a) n"),
+                )
+
+        def load_words(e0, e1):
+            nc.sync.dma_start(
+                out=words[:, PASSES * e0 : PASSES * e1, :].bitcast(I32),
+                in_=ww32[e0:e1, :, :, :].rearrange("e a p n -> p (e a) n"),
+            )
+
+        raws = {}
+        for i, (a, t0, w) in enumerate(LOADS):
             raw = held.tile([P, 4, w], F32, name=f"raw{i}")
             nc.sync.dma_start(out=raw[:], in_=xT[512 * a : 512 * (a + 1), t0 : t0 + w].rearrange("(p j) w -> p j w", j=4))
-            raws.append(raw)
-            if i == 1:
-                nc.sync.dma_start(offsets[:], offs)
-            if i == 2:
-                for q in range(4):
-                    nc.sync.dma_start(
-                        out=wscale[32 * q : 32 * q + 4, :, :].bitcast(I32),
-                        in_=ws32[:, :, 4 * q : 4 * q + 4, :].rearrange("e a q n -> q (e a) n"),
-                    )
-        ww32 = w_words.bitcast(I32)
-        for h in range(4):
-            nc.sync.dma_start(
-                out=words[:, 8 * h : 8 * h + 8, :].bitcast(I32),
-                in_=ww32[2 * h : 2 * h + 2, :, :, :].rearrange("e a p n -> p (e a) n"),
-            )
-        nc.sync.dma_start(out=bias[:], in_=b)
-        nc.sync.dma_start(out=gates[:], in_=gate)
+            raws[i] = raw
+            for what, at in [["offs",1],["scales",12],[[0,2],12],[[2,4],12],[[4,6],12],[[6,8],12],["bias",12],["gate",12]]:
+                if at == i:
+                    if what == "offs":
+                        nc.sync.dma_start(offsets[:], offs)
+                    elif what == "scales":
+                        load_scales()
+                    elif what == "gate":
+                        nc.sync.dma_start(out=gates[:], in_=gate)
+                    elif what == "bias":
+                        nc.sync.dma_start(out=bias[:], in_=b)
+                    else:
+                        load_words(*what)
 
-        def gather(a, s0, s1):
-            idx = offsets[:, s0 // 16 : s1 // 16]
-            nc.vector.tensor_copy(gcodes[a][:, s0:s1], codes[a][:].indirect(idx))
-            if a >= 2:
-                dst, src = (gpacked, packed) if a == 2 else (gscales[3], last)
-                nc.vector.tensor_copy(dst[:, s0:s1], src[:].indirect(idx))
+        def raw_of(a, t0, w):
+            for i, (la, lt, lw) in enumerate(LOADS):
+                if la == a and lt <= t0 and t0 + w <= lt + lw:
+                    return raws[i][:, :, t0 - lt : t0 - lt + w]
 
         def quantise(i):
-            a, t0, w, eng = chunks[i]
+            a, t0, w, eng = UNITS[i]
             grouped = held.tile([P, w, 4], BF16, name=f"grouped{i}", align_bytes=64)
             dst = grouped[:].rearrange("p (c i) t -> p c t i", i=4)
-            src = raws[i][:].rearrange("p t (c i) -> p c t i", i=4)
+            src = raw_of(a, t0, w).rearrange("p t (c i) -> p c t i", i=4)
             if eng == "s":
                 nc.scalar.activation(dst, src, ACT.Copy)
             else:
                 nc.vector.tensor_copy(dst, src)
             nc.vector.quantize_mx(
                 out=codes[a][:, t0 : t0 + w].bitcast(FP8X4),
-                scales=(last[:, t0 : t0 + w] if a == 3 else packed[4 * a :, t0 : t0 + w]),
+                scales=packed[ROW[a] :, t0 : t0 + w],
                 in_=grouped[:].rearrange("p w t -> p (w t)"),
             )
 
-        for i in range(len(chunks)):
-            quantise(i)
-            a, t0, w, eng = chunks[i]
-            if t0 + w == T and a < PASSES - 1:
-                gather(a, 0, 768)
-                gather(a, 768, 1536)
+        def gather(window, to, s0, s1):
+            nc.vector.tensor_copy(to[:, s0:s1], window[:].indirect(offsets[:, s0 // 16 : s1 // 16]))
 
-        for a in (1, 2):
-            nc.sync.dma_start(out=gscales[a][0:112, :].bitcast(I32), in_=gpacked[4 * a : 4 * a + 112, :].bitcast(I32))
+        for i in range(len(UNITS)):
+            quantise(i)
+            a, t0, w, eng = UNITS[i]
+            if t0 + w == T and a < PASSES - 1:
+                for s0, s1 in ((0, 768), (768, 1536)):
+                    gather(codes[a], gcodes[a], s0, s1)
 
         expert = [e for e in range(E) for _ in range(COUNTS[e] // 128)]
         starts = [sum(COUNTS[:e]) for e in range(E + 1)]
-        for i in range(3):
-            s0, s1 = 512 * i, 512 * i + 512
-            gather(PASSES - 1, s0, s1)
-            for g in range(4 * i, 4 * i + 4):
+        for s0, s1 in SLICES:
+            gather(packed, gpacked, s0, s1)
+            for a in range(3):
+                nc.sync.dma_start(out=moved[a][0:112, s0:s1].bitcast(I32), in_=gpacked[ROW[a] : ROW[a] + 112, s0:s1].bitcast(I32))
+        for s0, s1 in SLICES:
+            gather(codes[3], gcodes[3], s0, s1)
+            for g in range(s0 // 128, s1 // 128):
                 e = expert[g]
                 cols = slice(128 * g, 128 * g + 128)
                 for a in range(PASSES):
                     nc.tensor.matmul_mx(
-                        out=banks[i][:, 128 * (g - 4 * i) : 128 * (g - 4 * i) + 128],
+                        out=banks[g // 4][:, 128 * (g % 4) : 128 * (g % 4) + 128],
                         lhsT=words[:, PASSES * e + a, :].bitcast(FP4X4),
                         lhsT_scale=wscale[:, PASSES * e + a, :],
                         rhs=gcodes[a][:, cols].bitcast(FP8X4),
@@ -130,9 +149,11 @@ def tile_moe_rag_lin_gelu_kernel(tc, xT, w_words, w_scales, b, gate, offs, out):
                     )
             for e in range(E):
                 lo, hi = max(starts[e], s0), min(starts[e + 1], s1)
-                if lo < hi:
-                    nc.scalar.activation(y[:, lo:hi], banks[i][:, lo - s0 : hi - s0], ACT.Gelu_apprx_tanh, bias=bias[:, e : e + 1])
-        for i in range(3):
-            s0, s1 = 512 * i, 512 * i + 512
-            nc.vector.tensor_tensor(result[:].indirect(offsets[:, s0 // 16 : s1 // 16]), y[:, s0:s1], gates[:, s0:s1], MULT)
+                while lo < hi:
+                    end = min(hi, 512 * (lo // 512 + 1))
+                    nc.scalar.activation(y[:, lo:end], banks[lo // 512][:, lo % 512 : lo % 512 + end - lo], ACT.Gelu_apprx_tanh, bias=bias[:, e : e + 1])
+                    lo = end
+            nc.gpsimd.tensor_tensor(z[:, s0:s1], y[:, s0:s1], gates[:, s0:s1], MULT)
+        for s0, s1 in SLICES:
+            nc.vector.tensor_copy(result[:].indirect(offsets[:, s0 // 16 : s1 // 16]), z[:, s0:s1])
         nc.sync.dma_start(out=out, in_=result[:])

@@ -19,17 +19,17 @@ FLOPS = 2 * K * N * T
 
 LOADS = (
     (0, 0, 512), (0, 512, 512), (0, 1024, 512),
-    (1, 0, 512), (1, 512, 512), (1, 1024, 512),
-    (2, 0, 512), (2, 512, 512), (2, 1024, 512),
-    (3, 0, 512), (3, 512, 512), (3, 1024, 256), (3, 1280, 256),
+    (1, 0, 768), (1, 768, 768),
+    (2, 0, 768), (2, 768, 768),
+    (3, 0, 768), (3, 768, 512), (3, 1280, 256),
 )
 UNITS = (
-    (0, 0, 512, "s"), (0, 512, 512, "s"), (0, 1024, 256, "s"), (0, 1280, 256, "v"),
-    (1, 0, 512, "s"), (1, 512, 512, "s"), (1, 1024, 256, "s"), (1, 1280, 256, "v"),
-    (2, 0, 512, "s"), (2, 512, 512, "s"), (2, 1024, 256, "s"), (2, 1280, 256, "v"),
-    (3, 0, 512, "s"), (3, 512, 512, "s"), (3, 1024, 256, "s"), (3, 1280, 128, "s"), (3, 1408, 128, "v"),
+    (0, 0, 512, "v"), (0, 512, 512, "s"), (0, 1024, 256, "v"), (0, 1280, 256, "s"),
+    (1, 0, 512, "s"), (1, 512, 256, "v"), (1, 768, 512, "s"), (1, 1280, 256, "v"),
+    (2, 0, 512, "s"), (2, 512, 256, "v"), (2, 768, 512, "s"), (2, 1280, 256, "v"),
+    (3, 0, 512, "s"), (3, 512, 256, "v"), (3, 768, 256, "s"), (3, 1024, 256, "v"), (3, 1280, 128, "s"), (3, 1408, 128, "v"),
 )
-SLICES = ((0, 256), (256, 896), (896, 1536))
+SLICES = ((0, 512), (512, 1024), (1024, 1536))
 
 
 def tile_moe_rag_lin_gelu_kernel(tc, xT, w_words, w_scales, b, gate, offs, out):
@@ -52,7 +52,6 @@ def tile_moe_rag_lin_gelu_kernel(tc, xT, w_words, w_scales, b, gate, offs, out):
         gcodes = [held.tile([P, T], U32, name=f"gcodes{a}", align_bytes=64) for a in range(PASSES)]
         gscales = moved + [gpacked]
         y = held.tile([P, T], F32, name="y")
-        z = held.tile([P, T], F32, name="z")
         result = held.tile([P, T], F32, name="result")
         banks = [psum.tile([P, 512], F32, name=f"bank{i}") for i in range(3)]
 
@@ -83,14 +82,14 @@ def tile_moe_rag_lin_gelu_kernel(tc, xT, w_words, w_scales, b, gate, offs, out):
             raw = held.tile([P, 4, w], F32, name=f"raw{i}")
             nc.sync.dma_start(out=raw[:], in_=xT[512 * a : 512 * (a + 1), t0 : t0 + w].rearrange("(p j) w -> p j w", j=4))
             raws[i] = raw
-            for what, at in [["offs",1],["scales",12],[[0,2],12],[[2,4],12],[[4,6],12],[[6,8],12],["bias",12],["gate",12]]:
+            for what, at in [["offs",1],["bias",1],["scales",9],[[0,4],9],[["gate",0,512],9],[[4,6],9],[["gate",512,1024],9],[[6,8],9],[["gate",1024,1536],9]]:
                 if at == i:
                     if what == "offs":
                         nc.sync.dma_start(offsets[:], offs)
                     elif what == "scales":
                         load_scales()
-                    elif what == "gate":
-                        nc.sync.dma_start(out=gates[:], in_=gate)
+                    elif what[0] == "gate":
+                        nc.sync.dma_start(out=gates[:, what[1] : what[2]], in_=gate[:, what[1] : what[2]])
                     elif what == "bias":
                         nc.sync.dma_start(out=bias[:], in_=b)
                     else:
@@ -128,10 +127,10 @@ def tile_moe_rag_lin_gelu_kernel(tc, xT, w_words, w_scales, b, gate, offs, out):
 
         expert = [e for e in range(E) for _ in range(COUNTS[e] // 128)]
         starts = [sum(COUNTS[:e]) for e in range(E + 1)]
-        for s0, s1 in SLICES:
+        for s0, s1 in ((0, 512), (512, 1536)):
             gather(packed, gpacked, s0, s1)
             for a in range(3):
-                nc.sync.dma_start(out=moved[a][0:112, s0:s1].bitcast(I32), in_=gpacked[ROW[a] : ROW[a] + 112, s0:s1].bitcast(I32))
+                (nc.sync, nc.scalar, nc.sync)[a].dma_start(out=moved[a][0:112, s0:s1].bitcast(I32), in_=gpacked[ROW[a] : ROW[a] + 112, s0:s1].bitcast(I32))
         for s0, s1 in SLICES:
             gather(codes[3], gcodes[3], s0, s1)
             for g in range(s0 // 128, s1 // 128):
@@ -153,7 +152,6 @@ def tile_moe_rag_lin_gelu_kernel(tc, xT, w_words, w_scales, b, gate, offs, out):
                     end = min(hi, 512 * (lo // 512 + 1))
                     nc.scalar.activation(y[:, lo:end], banks[lo // 512][:, lo % 512 : lo % 512 + end - lo], ACT.Gelu_apprx_tanh, bias=bias[:, e : e + 1])
                     lo = end
-            nc.gpsimd.tensor_tensor(z[:, s0:s1], y[:, s0:s1], gates[:, s0:s1], MULT)
         for s0, s1 in SLICES:
-            nc.vector.tensor_copy(result[:].indirect(offsets[:, s0 // 16 : s1 // 16]), z[:, s0:s1])
+            nc.vector.tensor_tensor(result[:].indirect(offsets[:, s0 // 16 : s1 // 16]), y[:, s0:s1], gates[:, s0:s1], MULT)
         nc.sync.dma_start(out=out, in_=result[:])

@@ -19,17 +19,17 @@ FLOPS = 2 * K * N * T
 
 LOADS = (
     (0, 0, 512), (0, 512, 512), (0, 1024, 512),
-    (1, 0, 768), (1, 768, 768),
-    (2, 0, 768), (2, 768, 768),
-    (3, 0, 768), (3, 768, 512), (3, 1280, 256),
+    (1, 0, 512), (1, 512, 512), (1, 1024, 512),
+    (2, 0, 512), (2, 512, 512), (2, 1024, 512),
+    (3, 0, 512), (3, 512, 512), (3, 1024, 512),
 )
 UNITS = (
     (0, 0, 512, "v"), (0, 512, 512, "s"), (0, 1024, 256, "v"), (0, 1280, 256, "s"),
-    (1, 0, 512, "s"), (1, 512, 256, "v"), (1, 768, 512, "s"), (1, 1280, 256, "v"),
-    (2, 0, 512, "s"), (2, 512, 256, "v"), (2, 768, 512, "s"), (2, 1280, 256, "v"),
-    (3, 0, 512, "s"), (3, 512, 256, "v"), (3, 768, 256, "s"), (3, 1024, 256, "v"), (3, 1280, 128, "s"), (3, 1408, 128, "v"),
+    (1, 0, 512, "s"), (1, 512, 512, "s"), (1, 1024, 512, "v"),
+    (2, 0, 512, "s"), (2, 512, 512, "s"), (2, 1024, 256, "s"), (2, 1280, 256, "v"),
+    (3, 0, 512, "s"), (3, 512, 256, "v"), (3, 768, 256, "s"), (3, 1024, 256, "s"), (3, 1280, 128, "s"), (3, 1408, 128, "v"),
 )
-SLICES = ((0, 512), (512, 1024), (1024, 1536))
+SLICES = ((0, 384), (384, 768), (768, 1152), (1152, 1536))
 
 
 def tile_moe_rag_lin_gelu_kernel(tc, xT, w_words, w_scales, b, gate, offs, out):
@@ -48,11 +48,9 @@ def tile_moe_rag_lin_gelu_kernel(tc, xT, w_words, w_scales, b, gate, offs, out):
         gpacked = held.tile([P, T], U8, name="gpacked", align_bytes=64)
         moved = [held.tile([P, T], U8, name=f"moved{a}", align_bytes=64) for a in range(3)]
         ROW = (4, 8, 12, 0)
-        codes = [held.tile([P, T], U32, name=f"codes{a}", align_bytes=64) for a in range(PASSES)]
         gcodes = [held.tile([P, T], U32, name=f"gcodes{a}", align_bytes=64) for a in range(PASSES)]
         gscales = moved + [gpacked]
         y = held.tile([P, T], F32, name="y")
-        result = held.tile([P, T], F32, name="result")
         banks = [psum.tile([P, 512], F32, name=f"bank{i}") for i in range(3)]
 
         nc.vector.memset(warm[:], 0.0)
@@ -82,7 +80,7 @@ def tile_moe_rag_lin_gelu_kernel(tc, xT, w_words, w_scales, b, gate, offs, out):
             raw = held.tile([P, 4, w], F32, name=f"raw{i}")
             nc.sync.dma_start(out=raw[:], in_=xT[512 * a : 512 * (a + 1), t0 : t0 + w].rearrange("(p j) w -> p j w", j=4))
             raws[i] = raw
-            for what, at in [["offs",1],["bias",1],["scales",9],[[0,4],9],[["gate",0,512],9],[[4,6],9],[["gate",512,1024],9],[[6,8],9],[["gate",1024,1536],9]]:
+            for what, at in [["offs",1],["bias",1],["scales",11],[[0,2],11],[[2,4],11],[[4,6],11],[[6,8],11],[["gate",0,1536],11]]:
                 if at == i:
                     if what == "offs":
                         nc.sync.dma_start(offsets[:], offs)
@@ -102,7 +100,10 @@ def tile_moe_rag_lin_gelu_kernel(tc, xT, w_words, w_scales, b, gate, offs, out):
 
         def quantise(i):
             a, t0, w, eng = UNITS[i]
-            grouped = held.tile([P, w, 4], BF16, name=f"grouped{i}", align_bytes=64)
+            if t0 == 0:
+                codes[a] = held.tile([P, T], U32, name=f"codes{a}", tag="codes", align_bytes=64)
+            tag = f"grouped{a}" if t0 == 0 or (a > 0 and eng == "v") else f"grouped{a}_{t0}"
+            grouped = held.tile([P, w, 4], BF16, name=f"grouped{i}", tag=tag, align_bytes=64)
             dst = grouped[:].rearrange("p (c i) t -> p c t i", i=4)
             src = raw_of(a, t0, w).rearrange("p t (c i) -> p c t i", i=4)
             if eng == "s":
@@ -118,6 +119,7 @@ def tile_moe_rag_lin_gelu_kernel(tc, xT, w_words, w_scales, b, gate, offs, out):
         def gather(window, to, s0, s1):
             nc.vector.tensor_copy(to[:, s0:s1], window[:].indirect(offsets[:, s0 // 16 : s1 // 16]))
 
+        codes = {}
         for i in range(len(UNITS)):
             quantise(i)
             a, t0, w, eng = UNITS[i]
@@ -127,10 +129,10 @@ def tile_moe_rag_lin_gelu_kernel(tc, xT, w_words, w_scales, b, gate, offs, out):
 
         expert = [e for e in range(E) for _ in range(COUNTS[e] // 128)]
         starts = [sum(COUNTS[:e]) for e in range(E + 1)]
-        for s0, s1 in ((0, 512), (512, 1536)):
+        for s0, s1 in ((0, 384), (384, 1536)):
             gather(packed, gpacked, s0, s1)
             for a in range(3):
-                (nc.sync, nc.scalar, nc.sync)[a].dma_start(out=moved[a][0:112, s0:s1].bitcast(I32), in_=gpacked[ROW[a] : ROW[a] + 112, s0:s1].bitcast(I32))
+                nc.sync.dma_start(out=moved[a][0:112, s0:s1].bitcast(I32), in_=gpacked[ROW[a] : ROW[a] + 112, s0:s1].bitcast(I32))
         for s0, s1 in SLICES:
             gather(codes[3], gcodes[3], s0, s1)
             for g in range(s0 // 128, s1 // 128):
@@ -152,6 +154,7 @@ def tile_moe_rag_lin_gelu_kernel(tc, xT, w_words, w_scales, b, gate, offs, out):
                     end = min(hi, 512 * (lo // 512 + 1))
                     nc.scalar.activation(y[:, lo:end], banks[lo // 512][:, lo % 512 : lo % 512 + end - lo], ACT.Gelu_apprx_tanh, bias=bias[:, e : e + 1])
                     lo = end
+        result = held.tile([P, T], F32, name="result", tag="codes", align_bytes=64)
         for s0, s1 in SLICES:
             nc.vector.tensor_tensor(result[:].indirect(offsets[:, s0 // 16 : s1 // 16]), y[:, s0:s1], gates[:, s0:s1], MULT)
         nc.sync.dma_start(out=out, in_=result[:])

import concourse.mybir as mybir

F32 = mybir.dt.float32
BF16 = mybir.dt.bfloat16
I32 = mybir.dt.int32
U32 = mybir.dt.uint32
U16 = mybir.dt.uint16
U8 = mybir.dt.uint8
FP8X4 = mybir.dt.float8_e4m3fn_x4
FP4X4 = mybir.dt.float4_e2m1fn_x4
ACT = mybir.ActivationFunctionType
MULT = mybir.AluOpType.mult

P = 128
K, T, E, N = 2048, 1536, 8, 128
COUNTS = (128, 128, 128, 128, 128, 384, 384, 128)
PASSES = K // 512
FLOPS = 2 * K * N * T

LOADS = (
    (0, 0, 512), (0, 512, 512), (0, 1024, 512),
    (1, 0, 512), (1, 512, 512), (1, 1024, 512),
    (2, 0, 512), (2, 512, 512), (2, 1024, 512),
    (3, 0, 512), (3, 512, 512), (3, 1024, 512),
)
UNITS = (
    (0, 0, 512, "v"), (0, 512, 512, "s"), (0, 1024, 256, "v"), (0, 1280, 256, "s"),
    (1, 0, 512, "s"), (1, 512, 512, "s"), (1, 1024, 512, "v"),
    (2, 0, 512, "s"), (2, 512, 512, "s"), (2, 1024, 256, "s"), (2, 1280, 256, "v"),
    (3, 0, 512, "s"), (3, 512, 256, "v"), (3, 768, 256, "s"), (3, 1024, 256, "s"), (3, 1280, 128, "s"), (3, 1408, 128, "v"),
)
SLICES = ((0, 384), (384, 768), (768, 1152), (1152, 1536))


def tile_moe_rag_lin_gelu_kernel(tc, xT, w_words, w_scales, b, gate, offs, out):
    nc = tc.nc
    with (
        tc.tile_pool(name="held", bufs=1) as held,
        tc.psum_pool(name="psum", bufs=1) as psum,
    ):
        offsets = held.tile([P, T // 16], U16, name="offsets")
        wscale = held.tile([P, E * PASSES, N], U8, name="wscale", align_bytes=64)
        words = held.tile([P, E * PASSES, 2 * N], U8, name="words", align_bytes=64)
        bias = held.tile([P, E], F32, name="bias")
        gates = held.tile([P, T], F32, name="gates")
        warm = held.tile([P, 1], F32, name="warm")
        packed = held.tile([P, T], U8, name="packed", align_bytes=64)
        gpacked = held.tile([P, T], U8, name="gpacked", align_bytes=64)
        moved = [held.tile([P, T], U8, name=f"moved{a}", align_bytes=64) for a in range(3)]
        ROW = (4, 8, 12, 0)
        gcodes = [held.tile([P, T], U32, name=f"gcodes{a}", align_bytes=64) for a in range(PASSES)]
        gscales = moved + [gpacked]
        y = held.tile([P, T], F32, name="y")
        banks = [psum.tile([P, 512], F32, name=f"bank{i}") for i in range(3)]

        nc.vector.memset(warm[:], 0.0)
        nc.scalar.activation(warm[:], warm[:], ACT.Gelu_apprx_tanh)
        nc.gpsimd.memset(packed[:].bitcast(I32), 0)
        nc.gpsimd.memset(wscale[:].rearrange("p c n -> p (c n)").bitcast(I32), 0)
        for tile in moved:
            nc.gpsimd.memset(tile[:].bitcast(I32), 0)
        ws32 = w_scales.bitcast(I32)
        ww32 = w_words.bitcast(I32)

        def load_scales():
            for q in range(4):
                nc.sync.dma_start(
                    out=wscale[32 * q : 32 * q + 4, :, :].bitcast(I32),
                    in_=ws32[:, :, 4 * q : 4 * q + 4, :].rearrange("e a q n -> q (e a) n"),
                )

        def load_words(e0, e1):
            nc.sync.dma_start(
                out=words[:, PASSES * e0 : PASSES * e1, :].bitcast(I32),
                in_=ww32[e0:e1, :, :, :].rearrange("e a p n -> p (e a) n"),
            )

        raws = {}
        for i, (a, t0, w) in enumerate(LOADS):
            raw = held.tile([P, 4, w], F32, name=f"raw{i}")
            nc.sync.dma_start(out=raw[:], in_=xT[512 * a : 512 * (a + 1), t0 : t0 + w].rearrange("(p j) w -> p j w", j=4))
            raws[i] = raw
            for what, at in [["offs",1],["bias",1],["scales",11],[[0,2],11],[[2,4],11],[[4,6],11],[[6,8],11],[["gate",0,1536],11]]:
                if at == i:
                    if what == "offs":
                        nc.sync.dma_start(offsets[:], offs)
                    elif what == "scales":
                        load_scales()
                    elif what[0] == "gate":
                        nc.sync.dma_start(out=gates[:, what[1] : what[2]], in_=gate[:, what[1] : what[2]])
                    elif what == "bias":
                        nc.sync.dma_start(out=bias[:], in_=b)
                    else:
                        load_words(*what)

        def raw_of(a, t0, w):
            for i, (la, lt, lw) in enumerate(LOADS):
                if la == a and lt <= t0 and t0 + w <= lt + lw:
                    return raws[i][:, :, t0 - lt : t0 - lt + w]

        def quantise(i):
            a, t0, w, eng = UNITS[i]
            if t0 == 0:
                codes[a] = held.tile([P, T], U32, name=f"codes{a}", tag="codes", align_bytes=64)
            tag = f"grouped{a}" if t0 == 0 or (a > 0 and eng == "v") else f"grouped{a}_{t0}"
            grouped = held.tile([P, w, 4], BF16, name=f"grouped{i}", tag=tag, align_bytes=64)
            dst = grouped[:].rearrange("p (c i) t -> p c t i", i=4)
            src = raw_of(a, t0, w).rearrange("p t (c i) -> p c t i", i=4)
            if eng == "s":
                nc.scalar.activation(dst, src, ACT.Copy)
            else:
                nc.vector.tensor_copy(dst, src)
            nc.vector.quantize_mx(
                out=codes[a][:, t0 : t0 + w].bitcast(FP8X4),
                scales=packed[ROW[a] :, t0 : t0 + w],
                in_=grouped[:].rearrange("p w t -> p (w t)"),
            )

        def gather(window, to, s0, s1):
            nc.vector.tensor_copy(to[:, s0:s1], window[:].indirect(offsets[:, s0 // 16 : s1 // 16]))

        codes = {}
        for i in range(len(UNITS)):
            quantise(i)
            a, t0, w, eng = UNITS[i]
            if t0 + w == T and a < PASSES - 1:
                for s0, s1 in ((0, 768), (768, 1536)):
                    gather(codes[a], gcodes[a], s0, s1)

        expert = [e for e in range(E) for _ in range(COUNTS[e] // 128)]
        starts = [sum(COUNTS[:e]) for e in range(E + 1)]
        for s0, s1 in ((0, 384), (384, 1536)):
            gather(packed, gpacked, s0, s1)
            for a in range(3):
                nc.sync.dma_start(out=moved[a][0:112, s0:s1].bitcast(I32), in_=gpacked[ROW[a] : ROW[a] + 112, s0:s1].bitcast(I32))
        for s0, s1 in SLICES:
            gather(codes[3], gcodes[3], s0, s1)
            for g in range(s0 // 128, s1 // 128):
                e = expert[g]
                cols = slice(128 * g, 128 * g + 128)
                for a in range(PASSES):
                    nc.tensor.matmul_mx(
                        out=banks[g // 4][:, 128 * (g % 4) : 128 * (g % 4) + 128],
                        lhsT=words[:, PASSES * e + a, :].bitcast(FP4X4),
                        lhsT_scale=wscale[:, PASSES * e + a, :],
                        rhs=gcodes[a][:, cols].bitcast(FP8X4),
                        rhs_scale=gscales[a][:, cols],
                        start=(a == 0),
                        stop=(a == PASSES - 1),
                    )
            for e in range(E):
                lo, hi = max(starts[e], s0), min(starts[e + 1], s1)
                while lo < hi:
                    end = min(hi, 512 * (lo // 512 + 1))
                    nc.scalar.activation(y[:, lo:end], banks[lo // 512][:, lo % 512 : lo % 512 + end - lo], ACT.Gelu_apprx_tanh, bias=bias[:, e : e + 1])
                    lo = end
        result = held.tile([P, T], F32, name="result", tag="codes", align_bytes=64)
        for s0, s1 in SLICES:
            nc.vector.tensor_tensor(result[:].indirect(offsets[:, s0 // 16 : s1 // 16]), y[:, s0:s1], gates[:, s0:s1], MULT)
        nc.sync.dma_start(out=out, in_=result[:])
